import numpy as np
import ml_dtypes


def mxq(x, axis, fmt="e4m3"):
    dtype, down = {"e4m3": (ml_dtypes.float8_e4m3fn, 7), "e5m2": (ml_dtypes.float8_e5m2, 14)}[fmt]
    v = np.moveaxis(np.asarray(x, np.float32).astype(ml_dtypes.bfloat16).astype(np.float64), axis, -1)
    blocks = v.reshape(v.shape[:-1] + (-1, 32))
    amax = np.abs(blocks).max(-1, keepdims=True)
    byte = np.maximum(np.where(amax > 0, np.frexp(amax)[1] - 1 + 127, 0) - down, 1)
    scale = np.exp2(byte - 127.0)
    codes = (blocks / scale).astype(np.float32).astype(dtype).astype(np.float64)
    return np.moveaxis((codes * scale).reshape(v.shape), -1, axis)


WIDE = False


def mx_kscale(k):
    if not WIDE:
        return np.ones(k)
    levels = np.array([10, -10, 5, -5, 0])
    if k % 512:
        return np.exp2(np.random.permutation(np.resize(levels, k // 32))).repeat(32)
    a = np.empty((k // 512, 16))
    for p in range(k // 512):
        a[p, :8] = np.random.permutation(np.resize(levels, 8))
        for g in range(8):
            far = levels[np.abs(levels - a[p, g]) >= 10]
            a[p, g + 8] = far[np.random.randint(len(far))]
    return np.exp2(a.ravel()).repeat(32)


def f64(x):
    return np.asarray(x).astype(np.float64)


def striped(idx):
    return np.tile(idx.reshape(-1, 16).T, (8, 1)).astype(np.uint16)


def unstriped(offs):
    return offs[:16].T.reshape(-1).astype(np.int64)


def striped8(idx):
    return np.concatenate([x.reshape(-1, 16).T for x in idx]).astype(np.uint16)


def runs(offs, k):
    lists = np.stack([offs[16 * r : 16 * r + 16].T.reshape(-1) for r in range(8)]).astype(np.int64)
    return lists[np.arange(k) % 512 // 64]


def pack_weight(w):
    k, n = w.shape
    w = f64(np.asarray(w, np.float32).astype(ml_dtypes.bfloat16)).reshape(k // 32, 32, n)
    amax = np.abs(w).max(1)
    byte = np.clip(np.where(amax > 0, np.frexp(amax)[1] - 1 + 127 - 7, 1), 1, 254)
    scaled = (w * np.exp2(127.0 - byte)[:, None, :]).reshape(k, n).astype(np.float32)
    words = np.ascontiguousarray(scaled.reshape(k // 512, 128, 4, n).transpose(0, 1, 3, 2)).astype(ml_dtypes.float8_e4m3fn).view(np.uint8)
    return words, np.ascontiguousarray(byte.astype(np.uint8).reshape(k // 512, 16, n))


def unpack_weight(words, scales):
    g, p, n, _ = words.shape
    vals = np.ascontiguousarray(words).view(ml_dtypes.float8_e4m3fn).astype(np.float64) * np.repeat(np.exp2(scales.astype(np.float64) - 127.0), 8, axis=1)[..., None]
    return vals.transpose(0, 1, 3, 2).reshape(g * 512, n)


E2M1 = np.array([0.0, 0.5, 1.0, 1.5, 2.0, 3.0, 4.0, 6.0, -0.0, -0.5, -1.0, -1.5, -2.0, -3.0, -4.0, -6.0])


def pack_fp4(w):
    k, n = w.shape
    w = f64(np.asarray(w, np.float32).astype(ml_dtypes.bfloat16)).reshape(k // 32, 32, n)
    amax = np.abs(w).max(1)
    mant, ex = np.frexp(amax / 6.0)
    byte = np.clip(np.where(amax > 0, np.where(mant > 0.5, ex, ex - 1) + 127, 1), 1, 254)
    scaled = (w * np.exp2(127.0 - byte)[:, None, :]).reshape(k, n).astype(np.float32)
    c = np.ascontiguousarray(scaled.reshape(k // 512, 128, 4, n).transpose(0, 1, 3, 2)).astype(ml_dtypes.float4_e2m1fn).view(np.uint8) & 0xF
    words = (c[..., 0::2] | (c[..., 1::2] << 4)).reshape(k // 512, 128, 2 * n)
    return np.ascontiguousarray(words), np.ascontiguousarray(byte.astype(np.uint8).reshape(k // 512, 16, n))


def unpack_fp4(words, scales):
    g, _, n = scales.shape
    words = np.ascontiguousarray(words).reshape(g, 128, n, 2)
    nib = np.empty((g, 128, n, 4), np.uint8)
    nib[..., 0::2] = words & 0xF
    nib[..., 1::2] = words >> 4
    vals = E2M1[nib] * np.repeat(np.exp2(scales.astype(np.float64) - 127.0), 8, axis=1)[..., None]
    return vals.transpose(0, 1, 3, 2).reshape(g * 512, n)


def relu(v):
    return np.maximum(v, 0.0)

def planes(y):
    n, m = y.shape
    v = y.astype(np.float32).astype(ml_dtypes.bfloat16).astype(np.float64).reshape(n // 32, 32, m)
    top = np.abs(v).max(1)
    byte = np.clip(np.where(top > 0, np.frexp(top)[1] - 1 + 127 - 7, 1), 1, 254)
    codes = (v * np.exp2(127.0 - byte)[:, None, :]).reshape(n, m).astype(np.float32).astype(ml_dtypes.float8_e4m3fn).view(np.uint8)
    words = codes.reshape(n // 512, 128, 4, m).transpose(0, 1, 3, 2)
    return np.ascontiguousarray(words), np.ascontiguousarray(byte.astype(np.uint8).reshape(n // 512, 16, m))


K, T, S, H, C, U = 512, 2048, 512, 512, 512, 1024


def setup_inputs():
    n = np.random.standard_normal
    s = mx_kscale(K)[:, None]
    packed_xT = pack_weight(n((K, T)) * s)
    packed_w1 = pack_fp4(n((K, H)) / np.sqrt(K) / s)
    return {
        "x_words": packed_xT[0],
        "x_scales": packed_xT[1],
        "w1_words": packed_w1[0],
        "w1_scales": packed_w1[1],
        "gs": (np.random.uniform(0.5, 1.5, (K, 1)) / s).astype(np.float32),
        "old": n((C, U)).astype(np.float32),
        "offs": striped(np.random.permutation(T)[:S]),
        "cand": striped(np.random.permutation(T)[:C]),
        "slot": striped8(np.stack([np.random.permutation(U)[:S] for _ in range(8)])),
    }


def reference(x_words, x_scales, w1_words, w1_scales, gs, old, offs, cand, slot):
    x_cand = unpack_weight(x_words, x_scales)[:, unstriped(cand)]
    xq = unpack_weight(x_words, x_scales)[:, unstriped(offs)]
    h = relu(unpack_fp4(w1_words, w1_scales).T @ xq)
    z = f64(gs) * h
    s = 0.0625 * ((x_cand.T @ mxq(z, 0, "e4m3")))
    nw = np.minimum(s, f64(old)[np.arange(C)[:, None], runs(slot, C)] + 0.5)
    out = f64(old).copy()
    out[np.arange(C)[:, None], runs(slot, C)] = nw
    return (out,) + planes(out)

@@ -1,0 +1,197 @@
+from contextlib import ExitStack
+
+import concourse.mybir as mybir
+
+K, T, S, H, C, U = 512, 2048, 512, 512, 512, 1024
+FLOPS = 2 * K * H * S + 2 * K * C * S
+
+F32 = mybir.dt.float32
+BF16 = mybir.dt.bfloat16
+I32 = mybir.dt.int32
+U32 = mybir.dt.uint32
+U16 = mybir.dt.uint16
+U8 = mybir.dt.uint8
+FP8X4 = mybir.dt.float8_e4m3fn_x4
+FP4X4 = mybir.dt.float4_e2m1fn_x4
+ALU = mybir.AluOpType
+COPY = mybir.ActivationFunctionType.Copy
+
+P = 128
+PACK = 4
+QUADS = 4
+CHUNK = 128
+TILE_ORDER = (2, 0, 1, 3)
+VECTOR_COLS = 704
+
+
+def load_scale_rows(queue, tile, scales):
+    words = scales.shape[2] // 4
+    for q in range(QUADS):
+        rows = scales[0, 4 * q : 4 * q + 4, :].bitcast(I32)
+        queue.dma_start(tile[32 * q : 32 * (q + 1), :].bitcast(I32), rows.unsqueeze(0).to_broadcast([8, 4, words]))
+
+
+def tile_picked_candput_none_po_kernel(
+    tc, x_words, x_scales, w1_words, w1_scales, gs, old, offs, cand, slot, out_0, out_1, out_2
+):
+    nc = tc.nc
+    with ExitStack() as ctx:
+        keep = ctx.enter_context(tc.tile_pool(name="keep", bufs=1))
+        psum = ctx.enter_context(tc.psum_pool(name="psum", bufs=1))
+
+        offs_list = keep.tile([P, S // 16], U16)
+        cand_list = keep.tile([P, C // 16], U16)
+        slot_list = keep.tile([P, S // 16], U16)
+        x_word_table = keep.tile([P, T], U32, align_bytes=64)
+        x_scale_table = keep.tile([P, T], U8, align_bytes=64)
+        w_words_raw = keep.tile([P, 2 * H], U8, align_bytes=64)
+        w_scales_raw = keep.tile([P, H], U8, align_bytes=64)
+        gains = keep.tile([P, PACK], F32)
+        pages = [keep.tile([P, U], F32, name="page%d" % t, tag="page%d" % t) for t in range(PACK)]
+
+        nc.sync.dma_start(offs_list[:], offs)
+        load_scale_rows(nc.sync, x_scale_table, x_scales)
+        nc.sync.dma_start(cand_list[:], cand)
+        nc.sync.dma_start(x_word_table[:].bitcast(I32), x_words[0].rearrange("p c r -> p (c r)").bitcast(I32))
+        nc.sync.dma_start(w_words_raw[:].bitcast(I32), w1_words[0].bitcast(I32))
+        load_scale_rows(nc.sync, w_scales_raw, w1_scales)
+        nc.sync.dma_start(gains[:], gs.rearrange("(p t) o -> p (t o)", t=PACK))
+        nc.sync.dma_start(slot_list[:], slot)
+        old_rows = old.rearrange("(p t) u -> p t u", t=PACK)
+        for t in TILE_ORDER:
+            nc.sync.dma_start(pages[t][:], old_rows[:, t, :])
+
+        w_words = keep.tile([P, 2 * H], U8, align_bytes=64)
+        w_scales = keep.tile([P, H], U8, align_bytes=64)
+        nc.scalar.copy(
+            w_words[:].bitcast(U16).rearrange("p (t m) -> p t m", t=PACK),
+            w_words_raw[:].bitcast(U16).rearrange("p (m t) -> p t m", t=PACK),
+        )
+        nc.gpsimd.tensor_copy(
+            w_scales[:].rearrange("p (t m) -> p t m", t=PACK),
+            w_scales_raw[:].rearrange("p (m t) -> p t m", t=PACK),
+        )
+
+        token_scales = keep.tile([P, S], U8, align_bytes=64)
+        token_words = keep.tile([P, S], U32, align_bytes=64)
+        cand_scales = keep.tile([P, C], U8, align_bytes=64)
+        cand_words = keep.tile([P, C], U32, align_bytes=64)
+        nc.vector.tensor_copy(token_scales[:], x_scale_table[:].indirect(offs_list[:]))
+        nc.vector.tensor_copy(
+            cand_scales[:].rearrange("p (t m) -> p m t", t=PACK), x_scale_table[:].indirect(cand_list[:])
+        )
+        nc.vector.tensor_copy(token_words[:], x_word_table[:].indirect(offs_list[:]))
+        nc.vector.tensor_copy(
+            cand_words[:].rearrange("p (t m) -> p m t", t=PACK), x_word_table[:].indirect(cand_list[:])
+        )
+
+        ceilings = {}
+        for t in TILE_ORDER:
+            ceilings[t] = keep.tile([P, S], F32, name="ceiling%d" % t)
+            nc.scalar.activation(ceilings[t][:], pages[t][:].indirect(slot_list[:]), COPY, bias=0.5)
+
+        z_rounded = keep.tile([P, S, PACK], BF16, align_bytes=64)
+        z_words = keep.tile([P, S], U32, align_bytes=64)
+        z_scales = keep.tile([P, S], U8, align_bytes=64)
+        gain_pattern = gains[:].unsqueeze(1).to_broadcast([P, CHUNK, PACK])
+
+        def make_z(c):
+            cols = slice(c * CHUNK, (c + 1) * CHUNK)
+            h_bank = psum.tile([P, PACK, CHUNK], F32, name="h_bank%d" % c, tag="bank%d" % c)
+            for t in range(PACK):
+                nc.tensor.matmul_mx(
+                    out=h_bank[:, t, :],
+                    lhsT=w_words[:, 2 * P * t : 2 * P * (t + 1)].bitcast(FP4X4),
+                    lhsT_scale=w_scales[:, P * t : P * (t + 1)],
+                    rhs=token_words[:, cols].bitcast(FP8X4),
+                    rhs_scale=token_scales[:, cols],
+                    start=True,
+                    stop=True,
+                )
+            nc.vector.scalar_tensor_tensor(
+                out=z_rounded[:, cols, :],
+                in0=h_bank[:].rearrange("p t n -> p n t"),
+                scalar=0.0,
+                in1=gain_pattern,
+                op0=ALU.max,
+                op1=ALU.mult,
+            )
+
+        def quantise_z(cols):
+            nc.vector.quantize_mx(
+                out=z_words[:, cols].bitcast(FP8X4),
+                scales=z_scales[:, cols],
+                in_=z_rounded[:, cols, :].rearrange("p n t -> p (n t)"),
+            )
+
+        def score(t, cols, bank_tag, new_tag):
+            width = cols.stop - cols.start
+            s_bank = psum.tile([P, width], F32, name="s_" + bank_tag, tag=bank_tag)
+            nc.tensor.matmul_mx(
+                out=s_bank[:],
+                lhsT=cand_words[:, P * t : P * (t + 1)].bitcast(FP8X4),
+                lhsT_scale=cand_scales[:, P * t : P * (t + 1)],
+                rhs=z_words[:, cols].bitcast(FP8X4),
+                rhs_scale=z_scales[:, cols],
+                start=True,
+                stop=True,
+            )
+            new_values = keep.tile([P, width], F32, name="new_" + bank_tag, tag=new_tag)
+            nc.vector.scalar_tensor_tensor(
+                out=new_values[:], in0=s_bank[:], scalar=0.0625, in1=ceilings[t][:, cols], op0=ALU.mult, op1=ALU.min
+            )
+            return new_values
+
+        def put(t, cols, new_values):
+            offsets = slot_list[:, cols.start // 16 : cols.stop // 16]
+            nc.vector.tensor_copy(pages[t][:].indirect(offsets), new_values[:])
+
+        out_rows = out_0.rearrange("(p t) u -> p t u", t=PACK)
+        page_rounded = keep.tile([P, U, PACK], BF16, align_bytes=64)
+
+        def finish(t):
+            nc.sync.dma_start(out_rows[:, t, :], pages[t][:])
+            nc.scalar.copy(page_rounded[:, :, t], pages[t][:])
+
+        first, second, third, last = TILE_ORDER
+        low, high, whole = slice(0, S // 2), slice(S // 2, S), slice(0, S)
+        make_z(0)
+        make_z(1)
+        make_z(2)
+        quantise_z(low)
+        make_z(3)
+        new_low = score(first, low, "bank4", "new_low")
+        quantise_z(high)
+        put(first, low, new_low)
+        new_high = score(first, high, "bank5", "new_high")
+        new_second = score(second, whole, "bank6", "new_second")
+        put(first, high, new_high)
+        finish(first)
+        new_third = score(third, whole, "bank7", "new_third")
+        put(second, whole, new_second)
+        finish(second)
+        put(third, whole, new_third)
+        finish(third)
+        new_last = score(last, whole, "bank0", "page%d" % first)
+        put(last, whole, new_last)
+        nc.sync.dma_start(out_rows[:, last, :], pages[last][:])
+        half = U // 2
+        nc.vector.tensor_copy(page_rounded[:, :half, last], pages[last][:, :half])
+        nc.vector.tensor_copy(page_rounded[:, half:VECTOR_COLS, last], pages[last][:, half:VECTOR_COLS])
+        nc.scalar.copy(page_rounded[:, VECTOR_COLS:, last], pages[last][:, VECTOR_COLS:])
+
+        out_words = keep.tile([P, U], U32, align_bytes=64)
+        out_scales = keep.tile([P, U], U8, align_bytes=64)
+        word_rows = out_1[0].rearrange("p c r -> p (c r)").bitcast(I32)
+        for h in range(2):
+            cols = slice(h * half, (h + 1) * half)
+            nc.vector.quantize_mx(
+                out=out_words[:, cols].bitcast(FP8X4),
+                scales=out_scales[:, cols],
+                in_=page_rounded[:, cols, :].rearrange("p c t -> p (c t)"),
+            )
+            nc.sync.dma_start(word_rows[:, cols], out_words[:, cols].bitcast(I32))
+        for q in range(QUADS):
+            nc.scalar.dma_start(
+                out_2[0, 4 * q : 4 * q + 4, :].bitcast(I32), out_scales[32 * q : 32 * q + 4, :].bitcast(I32)
+            )

@@ -24,11 +24,9 @@ TILE_ORDER = (2, 0, 1, 3)
 VECTOR_COLS = 704
 
 
-def load_scale_rows(queue, tile, scales):
-    words = scales.shape[2] // 4
+def load_live_scale_rows(queue, tile, scales):
     for q in range(QUADS):
-        rows = scales[0, 4 * q : 4 * q + 4, :].bitcast(I32)
-        queue.dma_start(tile[32 * q : 32 * (q + 1), :].bitcast(I32), rows.unsqueeze(0).to_broadcast([8, 4, words]))
+        queue.dma_start(tile[32 * q : 32 * q + 4, :].bitcast(I32), scales[0, 4 * q : 4 * q + 4, :].bitcast(I32))
 
 
 def tile_picked_candput_none_po_kernel(
@@ -49,16 +47,20 @@ def tile_picked_candput_none_po_kernel(
         gains = keep.tile([P, PACK], F32)
         pages = [keep.tile([P, U], F32, name="page%d" % t, tag="page%d" % t) for t in range(PACK)]
 
+        nc.vector.memset(x_scale_table[:, : T // 2].bitcast(I32), 0)
+        nc.gpsimd.memset(x_scale_table[:, T // 2 :].bitcast(I32), 0)
         nc.sync.dma_start(offs_list[:], offs)
-        load_scale_rows(nc.sync, x_scale_table, x_scales)
+        load_live_scale_rows(nc.sync, x_scale_table, x_scales)
         nc.sync.dma_start(cand_list[:], cand)
         nc.sync.dma_start(x_word_table[:].bitcast(I32), x_words[0].rearrange("p c r -> p (c r)").bitcast(I32))
         nc.sync.dma_start(w_words_raw[:].bitcast(I32), w1_words[0].bitcast(I32))
-        load_scale_rows(nc.sync, w_scales_raw, w1_scales)
-        nc.sync.dma_start(gains[:], gs.rearrange("(p t) o -> p (t o)", t=PACK))
+        nc.gpsimd.memset(w_scales_raw[:].bitcast(I32), 0)
+        load_live_scale_rows(nc.sync, w_scales_raw, w1_scales)
         nc.sync.dma_start(slot_list[:], slot)
         old_rows = old.rearrange("(p t) u -> p t u", t=PACK)
-        for t in TILE_ORDER:
+        nc.sync.dma_start(pages[TILE_ORDER[0]][:], old_rows[:, TILE_ORDER[0], :])
+        nc.sync.dma_start(gains[:], gs.rearrange("(p t) o -> p (t o)", t=PACK))
+        for t in TILE_ORDER[1:]:
             nc.sync.dma_start(pages[t][:], old_rows[:, t, :])
 
         w_words = keep.tile([P, 2 * H], U8, align_bytes=64)
@@ -183,8 +185,7 @@ def tile_picked_candput_none_po_kernel(
         out_words = keep.tile([P, U], U32, align_bytes=64)
         out_scales = keep.tile([P, U], U8, align_bytes=64)
         word_rows = out_1[0].rearrange("p c r -> p (c r)").bitcast(I32)
-        for h in range(2):
-            cols = slice(h * half, (h + 1) * half)
+        for cols in (slice(0, half), slice(half, 3 * U // 4), slice(3 * U // 4, U)):
             nc.vector.quantize_mx(
                 out=out_words[:, cols].bitcast(FP8X4),
                 scales=out_scales[:, cols],
@@ -192,6 +193,7 @@ def tile_picked_candput_none_po_kernel(
             )
             nc.sync.dma_start(word_rows[:, cols], out_words[:, cols].bitcast(I32))
         for q in range(QUADS):
-            nc.scalar.dma_start(
+            queue = nc.scalar if q < 3 else nc.sync
+            queue.dma_start(
                 out_2[0, 4 * q : 4 * q + 4, :].bitcast(I32), out_scales[32 * q : 32 * q + 4, :].bitcast(I32)
             )

from contextlib import ExitStack

import concourse.mybir as mybir

K, T, S, H, C, U = 512, 2048, 512, 512, 512, 1024
FLOPS = 2 * K * H * S + 2 * K * C * S

F32 = mybir.dt.float32
BF16 = mybir.dt.bfloat16
I32 = mybir.dt.int32
U32 = mybir.dt.uint32
U16 = mybir.dt.uint16
U8 = mybir.dt.uint8
FP8X4 = mybir.dt.float8_e4m3fn_x4
FP4X4 = mybir.dt.float4_e2m1fn_x4
ALU = mybir.AluOpType
COPY = mybir.ActivationFunctionType.Copy

P = 128
PACK = 4
QUADS = 4
CHUNK = 128
TILE_ORDER = (2, 0, 1, 3)
VECTOR_COLS = 704


def load_live_scale_rows(queue, tile, scales):
    for q in range(QUADS):
        queue.dma_start(tile[32 * q : 32 * q + 4, :].bitcast(I32), scales[0, 4 * q : 4 * q + 4, :].bitcast(I32))


def tile_picked_candput_none_po_kernel(
    tc, x_words, x_scales, w1_words, w1_scales, gs, old, offs, cand, slot, out_0, out_1, out_2
):
    nc = tc.nc
    with ExitStack() as ctx:
        keep = ctx.enter_context(tc.tile_pool(name="keep", bufs=1))
        psum = ctx.enter_context(tc.psum_pool(name="psum", bufs=1))

        offs_list = keep.tile([P, S // 16], U16)
        cand_list = keep.tile([P, C // 16], U16)
        slot_list = keep.tile([P, S // 16], U16)
        x_word_table = keep.tile([P, T], U32, align_bytes=64)
        x_scale_table = keep.tile([P, T], U8, align_bytes=64)
        w_words_raw = keep.tile([P, 2 * H], U8, align_bytes=64)
        w_scales_raw = keep.tile([P, H], U8, align_bytes=64)
        gains = keep.tile([P, PACK], F32)
        pages = [keep.tile([P, U], F32, name="page%d" % t, tag="page%d" % t) for t in range(PACK)]

        nc.vector.memset(x_scale_table[:, : T // 2].bitcast(I32), 0)
        nc.gpsimd.memset(x_scale_table[:, T // 2 :].bitcast(I32), 0)
        nc.sync.dma_start(offs_list[:], offs)
        load_live_scale_rows(nc.sync, x_scale_table, x_scales)
        nc.sync.dma_start(cand_list[:], cand)
        nc.sync.dma_start(x_word_table[:].bitcast(I32), x_words[0].rearrange("p c r -> p (c r)").bitcast(I32))
        nc.sync.dma_start(w_words_raw[:].bitcast(I32), w1_words[0].bitcast(I32))
        nc.gpsimd.memset(w_scales_raw[:].bitcast(I32), 0)
        load_live_scale_rows(nc.sync, w_scales_raw, w1_scales)
        nc.sync.dma_start(slot_list[:], slot)
        old_rows = old.rearrange("(p t) u -> p t u", t=PACK)
        nc.sync.dma_start(pages[TILE_ORDER[0]][:], old_rows[:, TILE_ORDER[0], :])
        nc.sync.dma_start(gains[:], gs.rearrange("(p t) o -> p (t o)", t=PACK))
        for t in TILE_ORDER[1:]:
            nc.sync.dma_start(pages[t][:], old_rows[:, t, :])

        w_words = keep.tile([P, 2 * H], U8, align_bytes=64)
        w_scales = keep.tile([P, H], U8, align_bytes=64)
        nc.scalar.copy(
            w_words[:].bitcast(U16).rearrange("p (t m) -> p t m", t=PACK),
            w_words_raw[:].bitcast(U16).rearrange("p (m t) -> p t m", t=PACK),
        )
        nc.gpsimd.tensor_copy(
            w_scales[:].rearrange("p (t m) -> p t m", t=PACK),
            w_scales_raw[:].rearrange("p (m t) -> p t m", t=PACK),
        )

        token_scales = keep.tile([P, S], U8, align_bytes=64)
        token_words = keep.tile([P, S], U32, align_bytes=64)
        cand_scales = keep.tile([P, C], U8, align_bytes=64)
        cand_words = keep.tile([P, C], U32, align_bytes=64)
        nc.vector.tensor_copy(token_scales[:], x_scale_table[:].indirect(offs_list[:]))
        nc.vector.tensor_copy(
            cand_scales[:].rearrange("p (t m) -> p m t", t=PACK), x_scale_table[:].indirect(cand_list[:])
        )
        nc.vector.tensor_copy(token_words[:], x_word_table[:].indirect(offs_list[:]))
        nc.vector.tensor_copy(
            cand_words[:].rearrange("p (t m) -> p m t", t=PACK), x_word_table[:].indirect(cand_list[:])
        )

        ceilings = {}
        for t in TILE_ORDER:
            ceilings[t] = keep.tile([P, S], F32, name="ceiling%d" % t)
            nc.scalar.activation(ceilings[t][:], pages[t][:].indirect(slot_list[:]), COPY, bias=0.5)

        z_rounded = keep.tile([P, S, PACK], BF16, align_bytes=64)
        z_words = keep.tile([P, S], U32, align_bytes=64)
        z_scales = keep.tile([P, S], U8, align_bytes=64)
        gain_pattern = gains[:].unsqueeze(1).to_broadcast([P, CHUNK, PACK])

        def make_z(c):
            cols = slice(c * CHUNK, (c + 1) * CHUNK)
            h_bank = psum.tile([P, PACK, CHUNK], F32, name="h_bank%d" % c, tag="bank%d" % c)
            for t in range(PACK):
                nc.tensor.matmul_mx(
                    out=h_bank[:, t, :],
                    lhsT=w_words[:, 2 * P * t : 2 * P * (t + 1)].bitcast(FP4X4),
                    lhsT_scale=w_scales[:, P * t : P * (t + 1)],
                    rhs=token_words[:, cols].bitcast(FP8X4),
                    rhs_scale=token_scales[:, cols],
                    start=True,
                    stop=True,
                )
            nc.vector.scalar_tensor_tensor(
                out=z_rounded[:, cols, :],
                in0=h_bank[:].rearrange("p t n -> p n t"),
                scalar=0.0,
                in1=gain_pattern,
                op0=ALU.max,
                op1=ALU.mult,
            )

        def quantise_z(cols):
            nc.vector.quantize_mx(
                out=z_words[:, cols].bitcast(FP8X4),
                scales=z_scales[:, cols],
                in_=z_rounded[:, cols, :].rearrange("p n t -> p (n t)"),
            )

        def score(t, cols, bank_tag, new_tag):
            width = cols.stop - cols.start
            s_bank = psum.tile([P, width], F32, name="s_" + bank_tag, tag=bank_tag)
            nc.tensor.matmul_mx(
                out=s_bank[:],
                lhsT=cand_words[:, P * t : P * (t + 1)].bitcast(FP8X4),
                lhsT_scale=cand_scales[:, P * t : P * (t + 1)],
                rhs=z_words[:, cols].bitcast(FP8X4),
                rhs_scale=z_scales[:, cols],
                start=True,
                stop=True,
            )
            new_values = keep.tile([P, width], F32, name="new_" + bank_tag, tag=new_tag)
            nc.vector.scalar_tensor_tensor(
                out=new_values[:], in0=s_bank[:], scalar=0.0625, in1=ceilings[t][:, cols], op0=ALU.mult, op1=ALU.min
            )
            return new_values

        def put(t, cols, new_values):
            offsets = slot_list[:, cols.start // 16 : cols.stop // 16]
            nc.vector.tensor_copy(pages[t][:].indirect(offsets), new_values[:])

        out_rows = out_0.rearrange("(p t) u -> p t u", t=PACK)
        page_rounded = keep.tile([P, U, PACK], BF16, align_bytes=64)

        def finish(t):
            nc.sync.dma_start(out_rows[:, t, :], pages[t][:])
            nc.scalar.copy(page_rounded[:, :, t], pages[t][:])

        first, second, third, last = TILE_ORDER
        low, high, whole = slice(0, S // 2), slice(S // 2, S), slice(0, S)
        make_z(0)
        make_z(1)
        make_z(2)
        quantise_z(low)
        make_z(3)
        new_low = score(first, low, "bank4", "new_low")
        quantise_z(high)
        put(first, low, new_low)
        new_high = score(first, high, "bank5", "new_high")
        new_second = score(second, whole, "bank6", "new_second")
        put(first, high, new_high)
        finish(first)
        new_third = score(third, whole, "bank7", "new_third")
        put(second, whole, new_second)
        finish(second)
        put(third, whole, new_third)
        finish(third)
        new_last = score(last, whole, "bank0", "page%d" % first)
        put(last, whole, new_last)
        nc.sync.dma_start(out_rows[:, last, :], pages[last][:])
        half = U // 2
        nc.vector.tensor_copy(page_rounded[:, :half, last], pages[last][:, :half])
        nc.vector.tensor_copy(page_rounded[:, half:VECTOR_COLS, last], pages[last][:, half:VECTOR_COLS])
        nc.scalar.copy(page_rounded[:, VECTOR_COLS:, last], pages[last][:, VECTOR_COLS:])

        out_words = keep.tile([P, U], U32, align_bytes=64)
        out_scales = keep.tile([P, U], U8, align_bytes=64)
        word_rows = out_1[0].rearrange("p c r -> p (c r)").bitcast(I32)
        for cols in (slice(0, half), slice(half, 3 * U // 4), slice(3 * U // 4, U)):
            nc.vector.quantize_mx(
                out=out_words[:, cols].bitcast(FP8X4),
                scales=out_scales[:, cols],
                in_=page_rounded[:, cols, :].rearrange("p c t -> p (c t)"),
            )
            nc.sync.dma_start(word_rows[:, cols], out_words[:, cols].bitcast(I32))
        for q in range(QUADS):
            queue = nc.scalar if q < 3 else nc.sync
            queue.dma_start(
                out_2[0, 4 * q : 4 * q + 4, :].bitcast(I32), out_scales[32 * q : 32 * q + 4, :].bitcast(I32)
            )
